import numpy as np
import ml_dtypes


def mxq(x, axis, fmt="e4m3"):
    dtype, down = {"e4m3": (ml_dtypes.float8_e4m3fn, 7), "e5m2": (ml_dtypes.float8_e5m2, 14)}[fmt]
    v = np.moveaxis(np.asarray(x, np.float32).astype(ml_dtypes.bfloat16).astype(np.float64), axis, -1)
    blocks = v.reshape(v.shape[:-1] + (-1, 32))
    amax = np.abs(blocks).max(-1, keepdims=True)
    byte = np.maximum(np.where(amax > 0, np.frexp(amax)[1] - 1 + 127, 0) - down, 1)
    scale = np.exp2(byte - 127.0)
    codes = (blocks / scale).astype(np.float32).astype(dtype).astype(np.float64)
    return np.moveaxis((codes * scale).reshape(v.shape), -1, axis)


WIDE = False


def mx_kscale(k):
    if not WIDE:
        return np.ones(k)
    levels = np.array([10, -10, 5, -5, 0])
    if k % 512:
        return np.exp2(np.random.permutation(np.resize(levels, k // 32))).repeat(32)
    a = np.empty((k // 512, 16))
    for p in range(k // 512):
        a[p, :8] = np.random.permutation(np.resize(levels, 8))
        for g in range(8):
            far = levels[np.abs(levels - a[p, g]) >= 10]
            a[p, g + 8] = far[np.random.randint(len(far))]
    return np.exp2(a.ravel()).repeat(32)


def f64(x):
    return np.asarray(x).astype(np.float64)


def striped(idx):
    return np.tile(idx.reshape(-1, 16).T, (8, 1)).astype(np.uint16)


def unstriped(offs):
    return offs[:16].T.reshape(-1).astype(np.int64)


E2M1 = np.array([0.0, 0.5, 1.0, 1.5, 2.0, 3.0, 4.0, 6.0, -0.0, -0.5, -1.0, -1.5, -2.0, -3.0, -4.0, -6.0])


def pack_weight(w, fmt):
    k, n = w.shape
    w = f64(np.asarray(w, np.float32).astype(ml_dtypes.bfloat16)).reshape(k // 32, 32, n)
    amax = np.abs(w).max(1)
    if fmt == "e4m3":
        byte = np.frexp(amax)[1] - 1 + 127 - 7
    else:
        mant, ex = np.frexp(amax / 6.0)
        byte = np.where(mant > 0.5, ex, ex - 1) + 127
    byte = np.clip(np.where(amax > 0, byte, 1), 1, 254)
    scaled = (w * np.exp2(127.0 - byte)[:, None, :]).reshape(k, n).astype(np.float32)
    by_word = np.ascontiguousarray(scaled.reshape(k // 512, 128, 4, n).transpose(0, 1, 3, 2))
    if fmt == "e4m3":
        words = by_word.astype(ml_dtypes.float8_e4m3fn).view(np.uint8)
    else:
        c = by_word.astype(ml_dtypes.float4_e2m1fn).view(np.uint8) & 0xF
        words = (c[..., 0::2] | (c[..., 1::2] << 4)).reshape(k // 512, 128, 2 * n)
    return np.ascontiguousarray(words), np.ascontiguousarray(byte.astype(np.uint8).reshape(k // 512, 16, n))


def unpack_weight(words, scales, fmt):
    g, _, n = scales.shape
    words = np.ascontiguousarray(words).reshape(g, 128, n, -1)
    if fmt == "e4m3":
        vals = words.view(ml_dtypes.float8_e4m3fn).astype(np.float64)
    else:
        nib = np.empty((g, 128, n, 4), np.uint8)
        nib[..., 0::2] = words & 0xF
        nib[..., 1::2] = words >> 4
        vals = E2M1[nib]
    vals = vals * np.repeat(np.exp2(scales.astype(np.float64) - 127.0), 8, axis=1)[..., None]
    return vals.transpose(0, 1, 3, 2).reshape(g * 512, n)


def gelu(v):
    return 0.5 * v * (1.0 + np.tanh(np.sqrt(2.0 / np.pi) * (v + 0.044715 * v**3)))


K, T, S, H, T2, P, N = 1536, 2048, 1024, 512, 2048, 512, 768

def setup_inputs():
    n = np.random.standard_normal
    s = mx_kscale(K)[:, None]
    u = mx_kscale(H)[:, None]
    tab_words, tab_scales = pack_weight(n((K, T)) * s, "e4m3")
    w4_words, w4_scales = pack_weight(n((H, N)) / np.sqrt(H) / u, "e2m1")
    perm = np.random.permutation(T2)
    return {
        "tab_words": tab_words, "tab_scales": tab_scales,
        "offs": striped(np.random.permutation(T)[:S]),
        "offs2": striped(np.random.permutation(T2)[:S]),
        "offs3": striped(perm[:P]),
        "offs4": striped(perm[P:2 * P]),
        "w1": (1.3 * n((K, H)) / np.sqrt(K) / s).astype(np.float32),
        "gain": (np.exp(0.3 * n(H)) * u[:, 0]).astype(np.float32),
        "wgs": np.exp(0.3 * n((128, S))).astype(np.float32),
        "page0": (n((H, T2)) * u).astype(np.float32),
        "swing": n((H, P)).astype(np.float32),
        "lane": np.random.uniform(0.5, 2.0, H).astype(np.float32),
        "w4_words": w4_words, "w4_scales": w4_scales,
        "base": n((N, T2)).astype(np.float32),
    }

def reference(tab_words, tab_scales, offs, offs2, offs3, offs4, w1, gain, wgs, page0, swing, lane, w4_words, w4_scales, base):
    v = unpack_weight(tab_words, tab_scales, "e4m3")[:, unstriped(offs)]
    w4 = unpack_weight(w4_words, w4_scales, "e2m1")
    x = mxq(f64(w1), 0, "e4m3").T @ v
    x = 0.5 * x * (1.0 + np.tanh(0.7978845608028654 * (x + 0.044715 * x * x * x)))
    h = f64(gain)[:, None] * x
    page = f64(page0).copy()
    page[:, unstriped(offs2)] = np.tile(f64(wgs), (H // 128, 1)) * h
    a = page[:, unstriped(offs3)]
    b = page[:, unstriped(offs4)]
    page[:, unstriped(offs3)] = f64(swing) * a + b
    page[:, unstriped(offs4)] = np.maximum(a, b)
    z = mxq(f64(lane)[:, None] * page, 0, "e4m3")
    return (w4.T @ z) + f64(base)

@@ -1,0 +1,251 @@
+from contextlib import ExitStack
+
+import concourse.mybir as mybir
+
+K, T, S, H, T2, PAIRS, N = 1536, 2048, 1024, 512, 2048, 512, 768
+FLOPS = 2 * K * H * S + 2 * H * N * T2
+
+F32 = mybir.dt.float32
+BF16 = mybir.dt.bfloat16
+I32 = mybir.dt.int32
+U32 = mybir.dt.uint32
+U16 = mybir.dt.uint16
+U8 = mybir.dt.uint8
+FP8X4 = mybir.dt.float8_e4m3fn_x4
+FP4X4 = mybir.dt.float4_e2m1fn_x4
+ALU = mybir.AluOpType
+ACT = mybir.ActivationFunctionType
+
+P = 128
+PACK = 4
+QUADS = 4
+QUAD = P // QUADS
+PASSES = K // (P * PACK)
+BANK = 512
+HALVES = S // BANK
+N_TILES = N // P
+CHUNKS = (256, 256, 512, 512, 512)
+GROUP_BANKS = 3
+SIDE = {(3, 1), (3, 3), (3, 5), (4, 0), (4, 2), (4, 4)}
+
+
+def tile_list_lane_changeover_features_kernel(
+    tc, tab_words, tab_scales, offs, offs2, offs3, offs4, w1, gain, wgs, page0, swing, lane, w4_words, w4_scales, base, out
+):
+    nc = tc.nc
+    with ExitStack() as ctx:
+        keep = ctx.enter_context(tc.tile_pool(name="keep", bufs=1))
+        stage = ctx.enter_context(tc.tile_pool(name="stage", bufs=PASSES))
+        pair = ctx.enter_context(tc.tile_pool(name="pair", bufs=2))
+        side = ctx.enter_context(tc.tile_pool(name="side", bufs=3))
+        psum = ctx.enter_context(tc.psum_pool(name="psum", bufs=8))
+
+        def load_list(src, name):
+            tile = keep.tile(list(src.shape), U16, name=name)
+            nc.sync.dma_start(tile[:], src)
+            return tile
+
+        def load_table_words(a):
+            tile = keep.tile([P, T], U32, name="tab_words%d" % a)
+            nc.sync.dma_start(tile[:].bitcast(I32), tab_words[a].rearrange("p t i -> p (t i)").bitcast(I32))
+            return tile
+
+        def load_w1(a):
+            tile = stage.tile([P, PACK, H], F32, name="w1_raw%d" % a, tag="stage")
+            rows = w1[a * P * PACK : (a + 1) * P * PACK, :]
+            nc.sync.dma_start(tile[:], rows.rearrange("(p j) c -> p j c", j=PACK))
+            return tile
+
+        def load_rows(src, i, name):
+            tile = keep.tile([P, src.shape[1]], F32, name=name)
+            nc.sync.dma_start(tile[:], src.rearrange("(p i) c -> i p c", i=PACK)[i])
+            return tile
+
+        def load_wgs(i, c0, c1):
+            tile = keep.tile([P, c1 - c0], F32, name="wgs%d_%d" % (i, c0))
+            rows = wgs.rearrange("(q i) j -> i q j", i=PACK)[i][:, c0:c1]
+            for quad in range(QUADS):
+                nc.sync.dma_start(tile[QUAD * quad : QUAD * (quad + 1), :], rows)
+            return tile
+
+        planes = keep.tile([P, T], U8, name="tab_planes")
+        nc.vector.memset(planes[:].bitcast(I32), 0)
+        idx = load_list(offs, "idx")
+        words = [load_table_words(0)]
+        w1_raw = [load_w1(0)]
+        for quad in range(QUADS):
+            nc.sync.dma_start(
+                planes[QUAD * quad : QUAD * quad + PACK * PASSES, :].bitcast(I32),
+                tab_scales[:, PACK * quad : PACK * (quad + 1), :].bitcast(I32),
+            )
+        words.append(load_table_words(1))
+        w1_raw.append(load_w1(1))
+        w1_raw.append(load_w1(2))
+        words.append(load_table_words(2))
+        idx2 = load_list(offs2, "idx2")
+        gain_t = keep.tile([P, PACK], F32, name="gain_t")
+        nc.gpsimd.dma_start(gain_t[:], gain.rearrange("(p i) -> p i", i=PACK))
+        w4_plane = keep.tile([P, N], U8, name="w4_plane", align_bytes=64)
+        nc.gpsimd.memset(w4_plane[:].bitcast(I32), 0)
+
+        wgs_t = {(0, 0): load_wgs(0, 0, BANK)}
+        page = [load_rows(page0, 0, "page0")]
+        wgs_t[(0, 1)] = load_wgs(0, BANK, S)
+        idx3 = load_list(offs3, "idx3")
+        idx4 = load_list(offs4, "idx4")
+        swing_t = [load_rows(swing, 0, "swing0")]
+        lane_t = keep.tile([P, PACK], F32, name="lane_t")
+        nc.sync.dma_start(lane_t[:], lane.rearrange("(p i) -> p i", i=PACK))
+        for i in range(1, PACK):
+            page.append(load_rows(page0, i, "page%d" % i))
+            wgs_t[i] = load_wgs(i, 0, S)
+            swing_t.append(load_rows(swing, i, "swing%d" % i))
+        w4_t = keep.tile([P, 2 * N], U8, name="w4_t", align_bytes=64)
+        nc.sync.dma_start(w4_t[:].bitcast(I32), w4_words[0].bitcast(I32))
+        for quad in range(QUADS):
+            nc.sync.dma_start(
+                w4_plane[QUAD * quad : QUAD * quad + PACK, :].bitcast(I32),
+                w4_scales[0][PACK * quad : PACK * (quad + 1), :].bitcast(I32),
+            )
+
+        picked = [keep.tile([P, S], U32, name="picked%d" % a, align_bytes=64) for a in range(PASSES)]
+        picked_planes = keep.tile([P, S], U8, name="picked_planes", align_bytes=64)
+        w1_bf = [keep.tile([P, PACK, P, PACK], BF16, name="w1_bf%d" % a, align_bytes=64) for a in range(PASSES)]
+        w1_codes = [keep.tile([P, H], U32, name="w1_codes%d" % a, align_bytes=64) for a in range(PASSES)]
+        w1_plane = [keep.tile([P, H], U8, name="w1_plane%d" % a, align_bytes=64) for a in range(PASSES)]
+        cols16 = BANK // 16
+
+        def quantise_w1(a, i0, i1):
+            nc.scalar.copy(
+                w1_bf[a][:, i0:i1].rearrange("p i m j -> p m j i"),
+                w1_raw[a][:].rearrange("p j (m i) -> p m j i", i=PACK)[:, :, :, i0:i1],
+            )
+            nc.vector.quantize_mx(
+                out=w1_codes[a][:, P * i0 : P * i1].bitcast(FP8X4),
+                scales=w1_plane[a][:, P * i0 : P * i1],
+                in_=w1_bf[a][:, i0:i1].rearrange("p i m j -> p (i m j)"),
+            )
+
+        last = PASSES - 1
+        for a in range(last):
+            nc.vector.tensor_copy(picked[a][:], words[a][:].indirect(idx[:]))
+            if a == 0:
+                nc.vector.tensor_copy(picked_planes[:], planes[:].indirect(idx[:]))
+            quantise_w1(a, 0, PACK)
+        quantise_w1(last, 0, 1)
+        for half in range(HALVES):
+            nc.vector.tensor_copy(
+                picked[last][:, BANK * half : BANK * (half + 1)],
+                words[last][:].indirect(idx[:, cols16 * half : cols16 * (half + 1)]),
+            )
+        quantise_w1(last, 1, PACK)
+
+        h = [keep.tile([P, S], F32, name="h%d" % i) for i in range(PACK)]
+        for i in range(PACK):
+            for half in range(HALVES):
+                cols = slice(BANK * half, BANK * (half + 1))
+                acc = psum.tile([P, BANK], F32, name="acc", tag="acc")
+                for a in range(PASSES):
+                    nc.tensor.matmul_mx(
+                        out=acc[:],
+                        lhsT=w1_codes[a][:, P * i : P * (i + 1)].bitcast(FP8X4),
+                        lhsT_scale=w1_plane[a][:, P * i : P * (i + 1)],
+                        rhs=picked[a][:, cols].bitcast(FP8X4),
+                        rhs_scale=picked_planes[PACK * a : P, cols],
+                        start=(a == 0),
+                        stop=(a == last),
+                    )
+                nc.scalar.activation(h[i][:, cols], acc[:], ACT.Gelu_apprx_tanh)
+                nc.scalar.activation(h[i][:, cols], h[i][:, cols], ACT.Copy, scale=gain_t[:, i : i + 1])
+
+        starts = [sum(CHUNKS[:c]) for c in range(len(CHUNKS))]
+        groups = []
+        for c, width in enumerate(CHUNKS):
+            per_group = GROUP_BANKS * BANK // width
+            for k0 in range(0, N_TILES, per_group):
+                groups.append((c, k0, per_group))
+        base_rows = base.rearrange("(k p) t -> p k t", p=P)
+        out_rows = out.rearrange("(k p) t -> p k t", p=P)
+        total = {}
+        for g, (c, k0, count) in enumerate(groups):
+            shape = [P, count, CHUNKS[c]]
+            if g < len(groups) - PASSES:
+                tile = keep.tile(shape, F32, name="total%d" % g)
+            else:
+                tile = stage.tile(shape, F32, name="total%d" % g, tag="stage")
+            nc.sync.dma_start(tile[:], base_rows[:, k0 : k0 + count, starts[c] : starts[c] + CHUNKS[c]])
+            total[(c, k0)] = tile
+
+        z_bf = [keep.tile([P, width, PACK], BF16, name="z_bf%d" % c, align_bytes=64) for c, width in enumerate(CHUNKS)]
+        for half in range(HALVES):
+            nc.vector.tensor_tensor(
+                page[0][:].indirect(idx2[:, cols16 * half : cols16 * (half + 1)]),
+                h[0][:, BANK * half : BANK * (half + 1)],
+                wgs_t[(0, half)][:],
+                ALU.mult,
+            )
+        for i in range(PACK):
+            a_cols = pair.tile([P, PAIRS], F32, name="a_cols")
+            b_cols = pair.tile([P, PAIRS], F32, name="b_cols")
+            swung = pair.tile([P, PAIRS], F32, name="swung", bufs=1)
+            larger = pair.tile([P, PAIRS], F32, name="larger", bufs=1)
+            nc.vector.tensor_copy(a_cols[:], page[i][:].indirect(idx3[:]))
+            nc.vector.tensor_copy(b_cols[:], page[i][:].indirect(idx4[:]))
+            nc.vector.tensor_tensor(swung[:], a_cols[:], swing_t[i][:], ALU.mult)
+            nc.vector.tensor_tensor(larger[:], a_cols[:], b_cols[:], ALU.max)
+            nc.vector.tensor_tensor(page[i][:].indirect(idx3[:]), swung[:], b_cols[:], ALU.add)
+            if i + 1 < PACK:
+                nc.vector.tensor_tensor(page[i + 1][:].indirect(idx2[:]), h[i + 1][:], wgs_t[i + 1][:], ALU.mult)
+            nc.vector.tensor_copy(page[i][:].indirect(idx4[:]), larger[:])
+            for c, width in enumerate(CHUNKS):
+                nc.scalar.activation(
+                    z_bf[c][:, :, i], page[i][:, starts[c] : starts[c] + width], ACT.Copy, scale=lane_t[:, i : i + 1]
+                )
+
+        z_codes = [keep.tile([P, width], U32, name="z_codes%d" % c, align_bytes=64) for c, width in enumerate(CHUNKS)]
+        z_plane = [keep.tile([P, width], U8, name="z_plane%d" % c, align_bytes=64) for c, width in enumerate(CHUNKS)]
+
+        def quantise_page(c):
+            nc.vector.quantize_mx(
+                out=z_codes[c][:].bitcast(FP8X4), scales=z_plane[c][:], in_=z_bf[c][:].rearrange("p t i -> p (t i)")
+            )
+
+        def finish(c):
+            width = CHUNKS[c]
+            per_bank = BANK // width
+            per_group = GROUP_BANKS * per_bank
+            for bank in range(N_TILES // per_bank):
+                acc = psum.tile([P, BANK], F32, name="acc", tag="acc")
+                for u in range(per_bank):
+                    k = bank * per_bank + u
+                    nc.tensor.matmul_mx(
+                        out=acc[:, width * u : width * (u + 1)],
+                        lhsT=w4_t[:, 2 * P * k : 2 * P * (k + 1)].bitcast(FP4X4),
+                        lhsT_scale=w4_plane[:, P * k : P * (k + 1)],
+                        rhs=z_codes[c][:].bitcast(FP8X4),
+                        rhs_scale=z_plane[c][:],
+                        start=True,
+                        stop=True,
+                    )
+                k0 = (bank // GROUP_BANKS) * per_group
+                u0 = bank * per_bank - k0
+                part = total[(c, k0)][:, u0 : u0 + per_bank, :].rearrange("p k t -> p (k t)")
+                if (c, bank) in SIDE:
+                    sums = side.tile([P, BANK], F32, name="sums")
+                    nc.scalar.copy(sums[:], acc[:])
+                    nc.gpsimd.tensor_tensor(part, sums[:], part, ALU.add)
+                else:
+                    nc.vector.tensor_tensor(part, acc[:], part, ALU.add)
+                cols = slice(starts[c], starts[c] + width)
+                if c == 0:
+                    nc.sync.dma_start(
+                        out_rows[:, k0 + u0 : k0 + u0 + per_bank, cols], total[(c, k0)][:, u0 : u0 + per_bank, :]
+                    )
+                elif bank % GROUP_BANKS == GROUP_BANKS - 1:
+                    nc.sync.dma_start(out_rows[:, k0 : k0 + per_group, cols], total[(c, k0)][:])
+
+        quantise_page(0)
+        for c in range(len(CHUNKS)):
+            if c + 1 < len(CHUNKS):
+                quantise_page(c + 1)
+            finish(c)

@@ -25,8 +25,8 @@ BANK = 512
 HALVES = S // BANK
 N_TILES = N // P
 CHUNKS = (256, 256, 512, 512, 512)
-GROUP_BANKS = 3
-SIDE = {(3, 1), (3, 3), (3, 5), (4, 0), (4, 2), (4, 4)}
+STAGE_TILES = 4
+SIDE = {(2, 4), (2, 5), (3, 4), (3, 5), (4, 5)}
 
 
 def tile_list_lane_changeover_features_kernel(
@@ -38,7 +38,7 @@ def tile_list_lane_changeover_features_kernel(
         stage = ctx.enter_context(tc.tile_pool(name="stage", bufs=PASSES))
         pair = ctx.enter_context(tc.tile_pool(name="pair", bufs=2))
         side = ctx.enter_context(tc.tile_pool(name="side", bufs=3))
-        psum = ctx.enter_context(tc.psum_pool(name="psum", bufs=8))
+        psum = ctx.enter_context(tc.psum_pool(name="psum", bufs=1))
 
         def load_list(src, name):
             tile = keep.tile(list(src.shape), U16, name=name)
@@ -46,7 +46,7 @@ def tile_list_lane_changeover_features_kernel(
             return tile
 
         def load_table_words(a):
-            tile = keep.tile([P, T], U32, name="tab_words%d" % a)
+            tile = keep.tile([P, T], U32, name="tab_words%d" % a, tag="tab_words%d" % a, align_bytes=64)
             nc.sync.dma_start(tile[:].bitcast(I32), tab_words[a].rearrange("p t i -> p (t i)").bitcast(I32))
             return tile
 
@@ -61,9 +61,9 @@ def tile_list_lane_changeover_features_kernel(
             nc.sync.dma_start(tile[:], src.rearrange("(p i) c -> i p c", i=PACK)[i])
             return tile
 
-        def load_wgs(i, c0, c1):
-            tile = keep.tile([P, c1 - c0], F32, name="wgs%d_%d" % (i, c0))
-            rows = wgs.rearrange("(q i) j -> i q j", i=PACK)[i][:, c0:c1]
+        def load_wgs(i):
+            tile = keep.tile([P, S], F32, name="wgs%d" % i)
+            rows = wgs.rearrange("(q i) j -> i q j", i=PACK)[i]
             for quad in range(QUADS):
                 nc.sync.dma_start(tile[QUAD * quad : QUAD * (quad + 1), :], rows)
             return tile
@@ -82,24 +82,24 @@ def tile_list_lane_changeover_features_kernel(
         w1_raw.append(load_w1(1))
         w1_raw.append(load_w1(2))
         words.append(load_table_words(2))
+        wgs_t = [load_wgs(0)]
         idx2 = load_list(offs2, "idx2")
         gain_t = keep.tile([P, PACK], F32, name="gain_t")
         nc.gpsimd.dma_start(gain_t[:], gain.rearrange("(p i) -> p i", i=PACK))
         w4_plane = keep.tile([P, N], U8, name="w4_plane", align_bytes=64)
         nc.gpsimd.memset(w4_plane[:].bitcast(I32), 0)
 
-        wgs_t = {(0, 0): load_wgs(0, 0, BANK)}
         page = [load_rows(page0, 0, "page0")]
-        wgs_t[(0, 1)] = load_wgs(0, BANK, S)
         idx3 = load_list(offs3, "idx3")
         idx4 = load_list(offs4, "idx4")
-        swing_t = [load_rows(swing, 0, "swing0")]
+        swing_t = []
         lane_t = keep.tile([P, PACK], F32, name="lane_t")
         nc.sync.dma_start(lane_t[:], lane.rearrange("(p i) -> p i", i=PACK))
         for i in range(1, PACK):
             page.append(load_rows(page0, i, "page%d" % i))
-            wgs_t[i] = load_wgs(i, 0, S)
-            swing_t.append(load_rows(swing, i, "swing%d" % i))
+            wgs_t.append(load_wgs(i))
+            swing_t.append(load_rows(swing, i - 1, "swing%d" % (i - 1)))
+        swing_t.append(load_rows(swing, PACK - 1, "swing%d" % (PACK - 1)))
         w4_t = keep.tile([P, 2 * N], U8, name="w4_t", align_bytes=64)
         nc.sync.dma_start(w4_t[:].bitcast(I32), w4_words[0].bitcast(I32))
         for quad in range(QUADS):
@@ -111,17 +111,20 @@ def tile_list_lane_changeover_features_kernel(
         picked = [keep.tile([P, S], U32, name="picked%d" % a, align_bytes=64) for a in range(PASSES)]
         picked_planes = keep.tile([P, S], U8, name="picked_planes", align_bytes=64)
         w1_bf = [keep.tile([P, PACK, P, PACK], BF16, name="w1_bf%d" % a, align_bytes=64) for a in range(PASSES)]
-        w1_codes = [keep.tile([P, H], U32, name="w1_codes%d" % a, align_bytes=64) for a in range(PASSES)]
         w1_plane = [keep.tile([P, H], U8, name="w1_plane%d" % a, align_bytes=64) for a in range(PASSES)]
+        w1_codes = {}
         cols16 = BANK // 16
 
-        def quantise_w1(a, i0, i1):
+        def quantise_w1(a, i0, i1, tag):
+            codes = keep.tile([P, P * (i1 - i0)], U32, name="w1_codes%d_%d" % (a, i0), tag=tag, align_bytes=64)
+            for i in range(i0, i1):
+                w1_codes[(a, i)] = codes[:, P * (i - i0) : P * (i - i0 + 1)]
             nc.scalar.copy(
                 w1_bf[a][:, i0:i1].rearrange("p i m j -> p m j i"),
                 w1_raw[a][:].rearrange("p j (m i) -> p m j i", i=PACK)[:, :, :, i0:i1],
             )
             nc.vector.quantize_mx(
-                out=w1_codes[a][:, P * i0 : P * i1].bitcast(FP8X4),
+                out=codes[:].bitcast(FP8X4),
                 scales=w1_plane[a][:, P * i0 : P * i1],
                 in_=w1_bf[a][:, i0:i1].rearrange("p i m j -> p (i m j)"),
             )
@@ -131,121 +134,137 @@ def tile_list_lane_changeover_features_kernel(
             nc.vector.tensor_copy(picked[a][:], words[a][:].indirect(idx[:]))
             if a == 0:
                 nc.vector.tensor_copy(picked_planes[:], planes[:].indirect(idx[:]))
-            quantise_w1(a, 0, PACK)
-        quantise_w1(last, 0, 1)
+            quantise_w1(a, 0, PACK, "w1_codes%d" % a)
+        quantise_w1(last, 0, 1, "w1_codes%d" % last)
         for half in range(HALVES):
             nc.vector.tensor_copy(
                 picked[last][:, BANK * half : BANK * (half + 1)],
                 words[last][:].indirect(idx[:, cols16 * half : cols16 * (half + 1)]),
             )
-        quantise_w1(last, 1, PACK)
+        quantise_w1(last, 1, PACK, "tab_words%d" % last)
 
-        h = [keep.tile([P, S], F32, name="h%d" % i) for i in range(PACK)]
-        for i in range(PACK):
+        def first_product(i):
+            h = keep.tile([P, S], F32, name="h%d" % i)
             for half in range(HALVES):
                 cols = slice(BANK * half, BANK * (half + 1))
-                acc = psum.tile([P, BANK], F32, name="acc", tag="acc")
+                acc = psum.tile([P, BANK], F32, name="acc", tag="bank%d" % half)
                 for a in range(PASSES):
                     nc.tensor.matmul_mx(
                         out=acc[:],
-                        lhsT=w1_codes[a][:, P * i : P * (i + 1)].bitcast(FP8X4),
+                        lhsT=w1_codes[(a, i)].bitcast(FP8X4),
                         lhsT_scale=w1_plane[a][:, P * i : P * (i + 1)],
                         rhs=picked[a][:, cols].bitcast(FP8X4),
                         rhs_scale=picked_planes[PACK * a : P, cols],
                         start=(a == 0),
                         stop=(a == last),
                     )
-                nc.scalar.activation(h[i][:, cols], acc[:], ACT.Gelu_apprx_tanh)
-                nc.scalar.activation(h[i][:, cols], h[i][:, cols], ACT.Copy, scale=gain_t[:, i : i + 1])
+                nc.scalar.activation(h[:, cols], acc[:], ACT.Gelu_apprx_tanh)
+            if i == 0:
+                nc.gpsimd.tensor_scalar(wgs_t[i][:], wgs_t[i][:], gain_t[:, i : i + 1], 0.0, ALU.mult, ALU.add)
+            else:
+                nc.scalar.activation(h[:], h[:], ACT.Copy, scale=gain_t[:, i : i + 1])
+            return h
 
         starts = [sum(CHUNKS[:c]) for c in range(len(CHUNKS))]
-        groups = []
-        for c, width in enumerate(CHUNKS):
-            per_group = GROUP_BANKS * BANK // width
-            for k0 in range(0, N_TILES, per_group):
-                groups.append((c, k0, per_group))
         base_rows = base.rearrange("(k p) t -> p k t", p=P)
         out_rows = out.rearrange("(k p) t -> p k t", p=P)
         total = {}
-        for g, (c, k0, count) in enumerate(groups):
-            shape = [P, count, CHUNKS[c]]
-            if g < len(groups) - PASSES:
-                tile = keep.tile(shape, F32, name="total%d" % g)
+
+        def load_base(pool, tag, c, k0, k1):
+            tile = pool.tile([P, k1 - k0, CHUNKS[c]], F32, name="total%d_%d" % (c, k0), tag=tag)
+            nc.sync.dma_start(tile[:], base_rows[:, k0:k1, starts[c] : starts[c] + CHUNKS[c]])
+            for k in range(k0, k1):
+                total[(c, k)] = (tile, k0)
+
+        for c, width in enumerate(CHUNKS):
+            if width < BANK:
+                load_base(keep, "total%d" % c, c, 0, N_TILES)
             else:
-                tile = stage.tile(shape, F32, name="total%d" % g, tag="stage")
-            nc.sync.dma_start(tile[:], base_rows[:, k0 : k0 + count, starts[c] : starts[c] + CHUNKS[c]])
-            total[(c, k0)] = tile
+                load_base(keep, "total%d" % c, c, STAGE_TILES, N_TILES)
+        for c, width in enumerate(CHUNKS):
+            if width == BANK:
+                load_base(stage, "stage", c, 0, STAGE_TILES)
 
         z_bf = [keep.tile([P, width, PACK], BF16, name="z_bf%d" % c, align_bytes=64) for c, width in enumerate(CHUNKS)]
-        for half in range(HALVES):
-            nc.vector.tensor_tensor(
-                page[0][:].indirect(idx2[:, cols16 * half : cols16 * (half + 1)]),
-                h[0][:, BANK * half : BANK * (half + 1)],
-                wgs_t[(0, half)][:],
-                ALU.mult,
-            )
+
+        def round_page(i, c):
+            cols = slice(starts[c], starts[c] + CHUNKS[c])
+            nc.scalar.activation(z_bf[c][:, :, i], page[i][:, cols], ACT.Copy, scale=lane_t[:, i : i + 1])
+
+        h = first_product(0)
+        nc.vector.tensor_tensor(page[0][:].indirect(idx2[:]), h[:], wgs_t[0][:], ALU.mult)
         for i in range(PACK):
+            if i + 1 < PACK:
+                h = first_product(i + 1)
             a_cols = pair.tile([P, PAIRS], F32, name="a_cols")
             b_cols = pair.tile([P, PAIRS], F32, name="b_cols")
             swung = pair.tile([P, PAIRS], F32, name="swung", bufs=1)
-            larger = pair.tile([P, PAIRS], F32, name="larger", bufs=1)
+            larger = pair.tile([P, PAIRS], F32, name="larger")
             nc.vector.tensor_copy(a_cols[:], page[i][:].indirect(idx3[:]))
             nc.vector.tensor_copy(b_cols[:], page[i][:].indirect(idx4[:]))
             nc.vector.tensor_tensor(swung[:], a_cols[:], swing_t[i][:], ALU.mult)
             nc.vector.tensor_tensor(larger[:], a_cols[:], b_cols[:], ALU.max)
             nc.vector.tensor_tensor(page[i][:].indirect(idx3[:]), swung[:], b_cols[:], ALU.add)
             if i + 1 < PACK:
-                nc.vector.tensor_tensor(page[i + 1][:].indirect(idx2[:]), h[i + 1][:], wgs_t[i + 1][:], ALU.mult)
+                nc.vector.tensor_tensor(page[i + 1][:].indirect(idx2[:]), h[:], wgs_t[i + 1][:], ALU.mult)
             nc.vector.tensor_copy(page[i][:].indirect(idx4[:]), larger[:])
-            for c, width in enumerate(CHUNKS):
-                nc.scalar.activation(
-                    z_bf[c][:, :, i], page[i][:, starts[c] : starts[c] + width], ACT.Copy, scale=lane_t[:, i : i + 1]
-                )
+            if i + 1 < PACK:
+                for c in range(len(CHUNKS)):
+                    round_page(i, c)
 
-        z_codes = [keep.tile([P, width], U32, name="z_codes%d" % c, align_bytes=64) for c, width in enumerate(CHUNKS)]
-        z_plane = [keep.tile([P, width], U8, name="z_plane%d" % c, align_bytes=64) for c, width in enumerate(CHUNKS)]
+        z_mx = {}
 
         def quantise_page(c):
+            round_page(PACK - 1, c)
+            codes = pair.tile([P, CHUNKS[c]], U32, name="z_codes", align_bytes=64)
+            plane = pair.tile([P, CHUNKS[c]], U8, name="z_plane", align_bytes=64)
             nc.vector.quantize_mx(
-                out=z_codes[c][:].bitcast(FP8X4), scales=z_plane[c][:], in_=z_bf[c][:].rearrange("p t i -> p (t i)")
+                out=codes[:].bitcast(FP8X4), scales=plane[:], in_=z_bf[c][:].rearrange("p t i -> p (t i)")
             )
+            z_mx[c] = (codes, plane)
 
-        def finish(c):
+        def finish(c, banks):
             width = CHUNKS[c]
             per_bank = BANK // width
-            per_group = GROUP_BANKS * per_bank
-            for bank in range(N_TILES // per_bank):
-                acc = psum.tile([P, BANK], F32, name="acc", tag="acc")
+            codes, plane = z_mx[c]
+            for bank in banks:
+                turn = sum(CHUNKS[:c]) * N_TILES // BANK + bank
+                acc = psum.tile([P, BANK], F32, name="acc", tag="bank%d" % (turn % 8))
                 for u in range(per_bank):
                     k = bank * per_bank + u
                     nc.tensor.matmul_mx(
                         out=acc[:, width * u : width * (u + 1)],
                         lhsT=w4_t[:, 2 * P * k : 2 * P * (k + 1)].bitcast(FP4X4),
                         lhsT_scale=w4_plane[:, P * k : P * (k + 1)],
-                        rhs=z_codes[c][:].bitcast(FP8X4),
-                        rhs_scale=z_plane[c][:],
+                        rhs=codes[:].bitcast(FP8X4),
+                        rhs_scale=plane[:],
                         start=True,
                         stop=True,
                     )
-                k0 = (bank // GROUP_BANKS) * per_group
-                u0 = bank * per_bank - k0
-                part = total[(c, k0)][:, u0 : u0 + per_bank, :].rearrange("p k t -> p (k t)")
+                k = bank * per_bank
+                tile, k0 = total[(c, k)]
+                part = tile[:, k - k0 : k - k0 + per_bank, :].rearrange("p k t -> p (k t)")
                 if (c, bank) in SIDE:
                     sums = side.tile([P, BANK], F32, name="sums")
                     nc.scalar.copy(sums[:], acc[:])
                     nc.gpsimd.tensor_tensor(part, sums[:], part, ALU.add)
                 else:
                     nc.vector.tensor_tensor(part, acc[:], part, ALU.add)
-                cols = slice(starts[c], starts[c] + width)
-                if c == 0:
+                k_end = k + per_bank
+                count = 1 if c == 2 else 2
+                if k_end % count == 0:
+                    cols = slice(starts[c], starts[c] + width)
                     nc.sync.dma_start(
-                        out_rows[:, k0 + u0 : k0 + u0 + per_bank, cols], total[(c, k0)][:, u0 : u0 + per_bank, :]
+                        out_rows[:, k_end - count : k_end, cols], tile[:, k_end - count - k0 : k_end - k0, :]
                     )
-                elif bank % GROUP_BANKS == GROUP_BANKS - 1:
-                    nc.sync.dma_start(out_rows[:, k0 : k0 + per_group, cols], total[(c, k0)][:])
 
         quantise_page(0)
-        for c in range(len(CHUNKS)):
-            if c + 1 < len(CHUNKS):
-                quantise_page(c + 1)
-            finish(c)
+        quantise_page(1)
+        finish(0, range(3))
+        quantise_page(2)
+        finish(1, range(3))
+        for c in (2, 3):
+            finish(c, range(STAGE_TILES))
+            quantise_page(c + 1)
+            finish(c, range(STAGE_TILES, N_TILES))
+        finish(4, range(N_TILES))

@@ -64,7 +64,7 @@ def tile_list_lane_changeover_features_kernel(
         def load_wgs(i):
             tile = keep.tile([P, S], F32, name="wgs%d" % i)
             rows = wgs.rearrange("(q i) j -> i q j", i=PACK)[i]
-            for quad in range(QUADS):
+            for quad in (0, 2, 1, 3):
                 nc.sync.dma_start(tile[QUAD * quad : QUAD * (quad + 1), :], rows)
             return tile
 
@@ -74,7 +74,7 @@ def tile_list_lane_changeover_features_kernel(
         words = [load_table_words(0)]
         w1_raw = [load_w1(0)]
         for quad in range(QUADS):
-            nc.sync.dma_start(
+            nc.gpsimd.dma_start(
                 planes[QUAD * quad : QUAD * quad + PACK * PASSES, :].bitcast(I32),
                 tab_scales[:, PACK * quad : PACK * (quad + 1), :].bitcast(I32),
             )
@@ -119,10 +119,11 @@ def tile_list_lane_changeover_features_kernel(
             codes = keep.tile([P, P * (i1 - i0)], U32, name="w1_codes%d_%d" % (a, i0), tag=tag, align_bytes=64)
             for i in range(i0, i1):
                 w1_codes[(a, i)] = codes[:, P * (i - i0) : P * (i - i0 + 1)]
-            nc.scalar.copy(
-                w1_bf[a][:, i0:i1].rearrange("p i m j -> p m j i"),
-                w1_raw[a][:].rearrange("p j (m i) -> p m j i", i=PACK)[:, :, :, i0:i1],
-            )
+            for i in range(i0, i1, 2):
+                nc.scalar.copy(
+                    w1_bf[a][:, i : i + 2].rearrange("p i m j -> p m j i"),
+                    w1_raw[a][:].rearrange("p j (m i) -> p m j i", i=PACK)[:, :, :, i : i + 2],
+                )
             nc.vector.quantize_mx(
                 out=codes[:].bitcast(FP8X4),
                 scales=w1_plane[a][:, P * i0 : P * i1],
@@ -135,13 +136,13 @@ def tile_list_lane_changeover_features_kernel(
             if a == 0:
                 nc.vector.tensor_copy(picked_planes[:], planes[:].indirect(idx[:]))
             quantise_w1(a, 0, PACK, "w1_codes%d" % a)
-        quantise_w1(last, 0, 1, "w1_codes%d" % last)
+        quantise_w1(last, 0, 2, "w1_codes%d" % last)
         for half in range(HALVES):
             nc.vector.tensor_copy(
                 picked[last][:, BANK * half : BANK * (half + 1)],
                 words[last][:].indirect(idx[:, cols16 * half : cols16 * (half + 1)]),
             )
-        quantise_w1(last, 1, PACK, "tab_words%d" % last)
+        quantise_w1(last, 2, PACK, "tab_words%d" % last)
 
         def first_product(i):
             h = keep.tile([P, S], F32, name="h%d" % i)

@@ -61,9 +61,9 @@ def tile_list_lane_changeover_features_kernel(
             nc.sync.dma_start(tile[:], src.rearrange("(p i) c -> i p c", i=PACK)[i])
             return tile
 
-        def load_wgs(i):
-            tile = keep.tile([P, S], F32, name="wgs%d" % i)
-            rows = wgs.rearrange("(q i) j -> i q j", i=PACK)[i]
+        def load_wgs(i, c0, c1):
+            tile = keep.tile([P, c1 - c0], F32, name="wgs%d_%d" % (i, c0))
+            rows = wgs.rearrange("(q i) j -> i q j", i=PACK)[i][:, c0:c1]
             for quad in (0, 2, 1, 3):
                 nc.sync.dma_start(tile[QUAD * quad : QUAD * (quad + 1), :], rows)
             return tile
@@ -78,11 +78,11 @@ def tile_list_lane_changeover_features_kernel(
                 planes[QUAD * quad : QUAD * quad + PACK * PASSES, :].bitcast(I32),
                 tab_scales[:, PACK * quad : PACK * (quad + 1), :].bitcast(I32),
             )
-        words.append(load_table_words(1))
         w1_raw.append(load_w1(1))
+        words.append(load_table_words(1))
         w1_raw.append(load_w1(2))
         words.append(load_table_words(2))
-        wgs_t = [load_wgs(0)]
+        wgs_first = [load_wgs(0, 0, BANK)]
         idx2 = load_list(offs2, "idx2")
         gain_t = keep.tile([P, PACK], F32, name="gain_t")
         nc.gpsimd.dma_start(gain_t[:], gain.rearrange("(p i) -> p i", i=PACK))
@@ -90,6 +90,8 @@ def tile_list_lane_changeover_features_kernel(
         nc.gpsimd.memset(w4_plane[:].bitcast(I32), 0)
 
         page = [load_rows(page0, 0, "page0")]
+        wgs_first.append(load_wgs(0, BANK, S))
+        wgs_t = {}
         idx3 = load_list(offs3, "idx3")
         idx4 = load_list(offs4, "idx4")
         swing_t = []
@@ -97,7 +99,7 @@ def tile_list_lane_changeover_features_kernel(
         nc.sync.dma_start(lane_t[:], lane.rearrange("(p i) -> p i", i=PACK))
         for i in range(1, PACK):
             page.append(load_rows(page0, i, "page%d" % i))
-            wgs_t.append(load_wgs(i))
+            wgs_t[i] = load_wgs(i, 0, S)
             swing_t.append(load_rows(swing, i - 1, "swing%d" % (i - 1)))
         swing_t.append(load_rows(swing, PACK - 1, "swing%d" % (PACK - 1)))
         w4_t = keep.tile([P, 2 * N], U8, name="w4_t", align_bytes=64)
@@ -161,9 +163,9 @@ def tile_list_lane_changeover_features_kernel(
                     )
                 nc.scalar.activation(h[:, cols], acc[:], ACT.Gelu_apprx_tanh)
             if i == 0:
-                nc.gpsimd.tensor_scalar(wgs_t[i][:], wgs_t[i][:], gain_t[:, i : i + 1], 0.0, ALU.mult, ALU.add)
-            else:
-                nc.scalar.activation(h[:], h[:], ACT.Copy, scale=gain_t[:, i : i + 1])
+                nc.gpsimd.tensor_scalar(wgs_first[0][:], wgs_first[0][:], gain_t[:, 0:1], 0.0, ALU.mult, ALU.add)
+            rest = h[:, BANK:] if i == 0 else h[:]
+            nc.scalar.activation(rest, rest, ACT.Copy, scale=gain_t[:, i : i + 1])
             return h
 
         starts = [sum(CHUNKS[:c]) for c in range(len(CHUNKS))]
@@ -193,7 +195,13 @@ def tile_list_lane_changeover_features_kernel(
             nc.scalar.activation(z_bf[c][:, :, i], page[i][:, cols], ACT.Copy, scale=lane_t[:, i : i + 1])
 
         h = first_product(0)
-        nc.vector.tensor_tensor(page[0][:].indirect(idx2[:]), h[:], wgs_t[0][:], ALU.mult)
+        for half in range(HALVES):
+            nc.vector.tensor_tensor(
+                page[0][:].indirect(idx2[:, cols16 * half : cols16 * (half + 1)]),
+                h[:, BANK * half : BANK * (half + 1)],
+                wgs_first[half][:],
+                ALU.mult,
+            )
         for i in range(PACK):
             if i + 1 < PACK:
                 h = first_product(i + 1)

@@ -71,8 +71,8 @@ def tile_list_lane_changeover_features_kernel(
         planes = keep.tile([P, T], U8, name="tab_planes")
         nc.vector.memset(planes[:].bitcast(I32), 0)
         idx = load_list(offs, "idx")
-        words = [load_table_words(0)]
         w1_raw = [load_w1(0)]
+        words = [load_table_words(0)]
         for quad in range(QUADS):
             nc.gpsimd.dma_start(
                 planes[QUAD * quad : QUAD * quad + PACK * PASSES, :].bitcast(I32),
@@ -80,14 +80,14 @@ def tile_list_lane_changeover_features_kernel(
             )
         w1_raw.append(load_w1(1))
         words.append(load_table_words(1))
+        gain_t = keep.tile([P, PACK], F32, name="gain_t")
+        nc.sync.dma_start(gain_t[:], gain.rearrange("(p i) -> p i", i=PACK))
         w1_raw.append(load_w1(2))
         words.append(load_table_words(2))
         wgs_first = [load_wgs(0, 0, BANK)]
         idx2 = load_list(offs2, "idx2")
-        gain_t = keep.tile([P, PACK], F32, name="gain_t")
-        nc.gpsimd.dma_start(gain_t[:], gain.rearrange("(p i) -> p i", i=PACK))
         w4_plane = keep.tile([P, N], U8, name="w4_plane", align_bytes=64)
-        nc.gpsimd.memset(w4_plane[:].bitcast(I32), 0)
+        nc.vector.memset(w4_plane[:].bitcast(I32), 0)
 
         page = [load_rows(page0, 0, "page0")]
         wgs_first.append(load_wgs(0, BANK, S))
@@ -207,11 +207,11 @@ def tile_list_lane_changeover_features_kernel(
                 h = first_product(i + 1)
             a_cols = pair.tile([P, PAIRS], F32, name="a_cols")
             b_cols = pair.tile([P, PAIRS], F32, name="b_cols")
-            swung = pair.tile([P, PAIRS], F32, name="swung", bufs=1)
+            swung = pair.tile([P, PAIRS], F32, name="swung")
             larger = pair.tile([P, PAIRS], F32, name="larger")
             nc.vector.tensor_copy(a_cols[:], page[i][:].indirect(idx3[:]))
             nc.vector.tensor_copy(b_cols[:], page[i][:].indirect(idx4[:]))
-            nc.vector.tensor_tensor(swung[:], a_cols[:], swing_t[i][:], ALU.mult)
+            nc.gpsimd.tensor_tensor(swung[:], a_cols[:], swing_t[i][:], ALU.mult)
             nc.vector.tensor_tensor(larger[:], a_cols[:], b_cols[:], ALU.max)
             nc.vector.tensor_tensor(page[i][:].indirect(idx3[:]), swung[:], b_cols[:], ALU.add)
             if i + 1 < PACK:
@@ -272,8 +272,9 @@ def tile_list_lane_changeover_features_kernel(
         finish(0, range(3))
         quantise_page(2)
         finish(1, range(3))
-        for c in (2, 3):
-            finish(c, range(STAGE_TILES))
-            quantise_page(c + 1)
-            finish(c, range(STAGE_TILES, N_TILES))
+        quantise_page(3)
+        finish(2, range(N_TILES))
+        finish(3, range(2))
+        quantise_page(4)
+        finish(3, range(2, N_TILES))
         finish(4, range(N_TILES))

from contextlib import ExitStack

import concourse.mybir as mybir

K, T, S, H, T2, PAIRS, N = 1536, 2048, 1024, 512, 2048, 512, 768
FLOPS = 2 * K * H * S + 2 * H * N * T2

F32 = mybir.dt.float32
BF16 = mybir.dt.bfloat16
I32 = mybir.dt.int32
U32 = mybir.dt.uint32
U16 = mybir.dt.uint16
U8 = mybir.dt.uint8
FP8X4 = mybir.dt.float8_e4m3fn_x4
FP4X4 = mybir.dt.float4_e2m1fn_x4
ALU = mybir.AluOpType
ACT = mybir.ActivationFunctionType

P = 128
PACK = 4
QUADS = 4
QUAD = P // QUADS
PASSES = K // (P * PACK)
BANK = 512
HALVES = S // BANK
N_TILES = N // P
CHUNKS = (256, 256, 512, 512, 512)
STAGE_TILES = 4
SIDE = {(2, 4), (2, 5), (3, 4), (3, 5), (4, 5)}


def tile_list_lane_changeover_features_kernel(
    tc, tab_words, tab_scales, offs, offs2, offs3, offs4, w1, gain, wgs, page0, swing, lane, w4_words, w4_scales, base, out
):
    nc = tc.nc
    with ExitStack() as ctx:
        keep = ctx.enter_context(tc.tile_pool(name="keep", bufs=1))
        stage = ctx.enter_context(tc.tile_pool(name="stage", bufs=PASSES))
        pair = ctx.enter_context(tc.tile_pool(name="pair", bufs=2))
        side = ctx.enter_context(tc.tile_pool(name="side", bufs=3))
        psum = ctx.enter_context(tc.psum_pool(name="psum", bufs=1))

        def load_list(src, name):
            tile = keep.tile(list(src.shape), U16, name=name)
            nc.sync.dma_start(tile[:], src)
            return tile

        def load_table_words(a):
            tile = keep.tile([P, T], U32, name="tab_words%d" % a, tag="tab_words%d" % a, align_bytes=64)
            nc.sync.dma_start(tile[:].bitcast(I32), tab_words[a].rearrange("p t i -> p (t i)").bitcast(I32))
            return tile

        def load_w1(a):
            tile = stage.tile([P, PACK, H], F32, name="w1_raw%d" % a, tag="stage")
            rows = w1[a * P * PACK : (a + 1) * P * PACK, :]
            nc.sync.dma_start(tile[:], rows.rearrange("(p j) c -> p j c", j=PACK))
            return tile

        def load_rows(src, i, name):
            tile = keep.tile([P, src.shape[1]], F32, name=name)
            nc.sync.dma_start(tile[:], src.rearrange("(p i) c -> i p c", i=PACK)[i])
            return tile

        def load_wgs(i, c0, c1):
            tile = keep.tile([P, c1 - c0], F32, name="wgs%d_%d" % (i, c0))
            rows = wgs.rearrange("(q i) j -> i q j", i=PACK)[i][:, c0:c1]
            for quad in (0, 2, 1, 3):
                nc.sync.dma_start(tile[QUAD * quad : QUAD * (quad + 1), :], rows)
            return tile

        planes = keep.tile([P, T], U8, name="tab_planes")
        nc.vector.memset(planes[:].bitcast(I32), 0)
        idx = load_list(offs, "idx")
        w1_raw = [load_w1(0)]
        words = [load_table_words(0)]
        for quad in range(QUADS):
            nc.gpsimd.dma_start(
                planes[QUAD * quad : QUAD * quad + PACK * PASSES, :].bitcast(I32),
                tab_scales[:, PACK * quad : PACK * (quad + 1), :].bitcast(I32),
            )
        w1_raw.append(load_w1(1))
        words.append(load_table_words(1))
        gain_t = keep.tile([P, PACK], F32, name="gain_t")
        nc.sync.dma_start(gain_t[:], gain.rearrange("(p i) -> p i", i=PACK))
        w1_raw.append(load_w1(2))
        words.append(load_table_words(2))
        wgs_first = [load_wgs(0, 0, BANK)]
        idx2 = load_list(offs2, "idx2")
        w4_plane = keep.tile([P, N], U8, name="w4_plane", align_bytes=64)
        nc.vector.memset(w4_plane[:].bitcast(I32), 0)

        page = [load_rows(page0, 0, "page0")]
        wgs_first.append(load_wgs(0, BANK, S))
        wgs_t = {}
        idx3 = load_list(offs3, "idx3")
        idx4 = load_list(offs4, "idx4")
        swing_t = []
        lane_t = keep.tile([P, PACK], F32, name="lane_t")
        nc.sync.dma_start(lane_t[:], lane.rearrange("(p i) -> p i", i=PACK))
        for i in range(1, PACK):
            page.append(load_rows(page0, i, "page%d" % i))
            wgs_t[i] = load_wgs(i, 0, S)
            swing_t.append(load_rows(swing, i - 1, "swing%d" % (i - 1)))
        swing_t.append(load_rows(swing, PACK - 1, "swing%d" % (PACK - 1)))
        w4_t = keep.tile([P, 2 * N], U8, name="w4_t", align_bytes=64)
        nc.sync.dma_start(w4_t[:].bitcast(I32), w4_words[0].bitcast(I32))
        for quad in range(QUADS):
            nc.sync.dma_start(
                w4_plane[QUAD * quad : QUAD * quad + PACK, :].bitcast(I32),
                w4_scales[0][PACK * quad : PACK * (quad + 1), :].bitcast(I32),
            )

        picked = [keep.tile([P, S], U32, name="picked%d" % a, align_bytes=64) for a in range(PASSES)]
        picked_planes = keep.tile([P, S], U8, name="picked_planes", align_bytes=64)
        w1_bf = [keep.tile([P, PACK, P, PACK], BF16, name="w1_bf%d" % a, align_bytes=64) for a in range(PASSES)]
        w1_plane = [keep.tile([P, H], U8, name="w1_plane%d" % a, align_bytes=64) for a in range(PASSES)]
        w1_codes = {}
        cols16 = BANK // 16

        def quantise_w1(a, i0, i1, tag):
            codes = keep.tile([P, P * (i1 - i0)], U32, name="w1_codes%d_%d" % (a, i0), tag=tag, align_bytes=64)
            for i in range(i0, i1):
                w1_codes[(a, i)] = codes[:, P * (i - i0) : P * (i - i0 + 1)]
            for i in range(i0, i1, 2):
                nc.scalar.copy(
                    w1_bf[a][:, i : i + 2].rearrange("p i m j -> p m j i"),
                    w1_raw[a][:].rearrange("p j (m i) -> p m j i", i=PACK)[:, :, :, i : i + 2],
                )
            nc.vector.quantize_mx(
                out=codes[:].bitcast(FP8X4),
                scales=w1_plane[a][:, P * i0 : P * i1],
                in_=w1_bf[a][:, i0:i1].rearrange("p i m j -> p (i m j)"),
            )

        last = PASSES - 1
        for a in range(last):
            nc.vector.tensor_copy(picked[a][:], words[a][:].indirect(idx[:]))
            if a == 0:
                nc.vector.tensor_copy(picked_planes[:], planes[:].indirect(idx[:]))
            quantise_w1(a, 0, PACK, "w1_codes%d" % a)
        quantise_w1(last, 0, 2, "w1_codes%d" % last)
        for half in range(HALVES):
            nc.vector.tensor_copy(
                picked[last][:, BANK * half : BANK * (half + 1)],
                words[last][:].indirect(idx[:, cols16 * half : cols16 * (half + 1)]),
            )
        quantise_w1(last, 2, PACK, "tab_words%d" % last)

        def first_product(i):
            h = keep.tile([P, S], F32, name="h%d" % i)
            for half in range(HALVES):
                cols = slice(BANK * half, BANK * (half + 1))
                acc = psum.tile([P, BANK], F32, name="acc", tag="bank%d" % half)
                for a in range(PASSES):
                    nc.tensor.matmul_mx(
                        out=acc[:],
                        lhsT=w1_codes[(a, i)].bitcast(FP8X4),
                        lhsT_scale=w1_plane[a][:, P * i : P * (i + 1)],
                        rhs=picked[a][:, cols].bitcast(FP8X4),
                        rhs_scale=picked_planes[PACK * a : P, cols],
                        start=(a == 0),
                        stop=(a == last),
                    )
                nc.scalar.activation(h[:, cols], acc[:], ACT.Gelu_apprx_tanh)
            if i == 0:
                nc.gpsimd.tensor_scalar(wgs_first[0][:], wgs_first[0][:], gain_t[:, 0:1], 0.0, ALU.mult, ALU.add)
            rest = h[:, BANK:] if i == 0 else h[:]
            nc.scalar.activation(rest, rest, ACT.Copy, scale=gain_t[:, i : i + 1])
            return h

        starts = [sum(CHUNKS[:c]) for c in range(len(CHUNKS))]
        base_rows = base.rearrange("(k p) t -> p k t", p=P)
        out_rows = out.rearrange("(k p) t -> p k t", p=P)
        total = {}

        def load_base(pool, tag, c, k0, k1):
            tile = pool.tile([P, k1 - k0, CHUNKS[c]], F32, name="total%d_%d" % (c, k0), tag=tag)
            nc.sync.dma_start(tile[:], base_rows[:, k0:k1, starts[c] : starts[c] + CHUNKS[c]])
            for k in range(k0, k1):
                total[(c, k)] = (tile, k0)

        for c, width in enumerate(CHUNKS):
            if width < BANK:
                load_base(keep, "total%d" % c, c, 0, N_TILES)
            else:
                load_base(keep, "total%d" % c, c, STAGE_TILES, N_TILES)
        for c, width in enumerate(CHUNKS):
            if width == BANK:
                load_base(stage, "stage", c, 0, STAGE_TILES)

        z_bf = [keep.tile([P, width, PACK], BF16, name="z_bf%d" % c, align_bytes=64) for c, width in enumerate(CHUNKS)]

        def round_page(i, c):
            cols = slice(starts[c], starts[c] + CHUNKS[c])
            nc.scalar.activation(z_bf[c][:, :, i], page[i][:, cols], ACT.Copy, scale=lane_t[:, i : i + 1])

        h = first_product(0)
        for half in range(HALVES):
            nc.vector.tensor_tensor(
                page[0][:].indirect(idx2[:, cols16 * half : cols16 * (half + 1)]),
                h[:, BANK * half : BANK * (half + 1)],
                wgs_first[half][:],
                ALU.mult,
            )
        for i in range(PACK):
            if i + 1 < PACK:
                h = first_product(i + 1)
            a_cols = pair.tile([P, PAIRS], F32, name="a_cols")
            b_cols = pair.tile([P, PAIRS], F32, name="b_cols")
            swung = pair.tile([P, PAIRS], F32, name="swung")
            larger = pair.tile([P, PAIRS], F32, name="larger")
            nc.vector.tensor_copy(a_cols[:], page[i][:].indirect(idx3[:]))
            nc.vector.tensor_copy(b_cols[:], page[i][:].indirect(idx4[:]))
            nc.gpsimd.tensor_tensor(swung[:], a_cols[:], swing_t[i][:], ALU.mult)
            nc.vector.tensor_tensor(larger[:], a_cols[:], b_cols[:], ALU.max)
            nc.vector.tensor_tensor(page[i][:].indirect(idx3[:]), swung[:], b_cols[:], ALU.add)
            if i + 1 < PACK:
                nc.vector.tensor_tensor(page[i + 1][:].indirect(idx2[:]), h[:], wgs_t[i + 1][:], ALU.mult)
            nc.vector.tensor_copy(page[i][:].indirect(idx4[:]), larger[:])
            if i + 1 < PACK:
                for c in range(len(CHUNKS)):
                    round_page(i, c)

        z_mx = {}

        def quantise_page(c):
            round_page(PACK - 1, c)
            codes = pair.tile([P, CHUNKS[c]], U32, name="z_codes", align_bytes=64)
            plane = pair.tile([P, CHUNKS[c]], U8, name="z_plane", align_bytes=64)
            nc.vector.quantize_mx(
                out=codes[:].bitcast(FP8X4), scales=plane[:], in_=z_bf[c][:].rearrange("p t i -> p (t i)")
            )
            z_mx[c] = (codes, plane)

        def finish(c, banks):
            width = CHUNKS[c]
            per_bank = BANK // width
            codes, plane = z_mx[c]
            for bank in banks:
                turn = sum(CHUNKS[:c]) * N_TILES // BANK + bank
                acc = psum.tile([P, BANK], F32, name="acc", tag="bank%d" % (turn % 8))
                for u in range(per_bank):
                    k = bank * per_bank + u
                    nc.tensor.matmul_mx(
                        out=acc[:, width * u : width * (u + 1)],
                        lhsT=w4_t[:, 2 * P * k : 2 * P * (k + 1)].bitcast(FP4X4),
                        lhsT_scale=w4_plane[:, P * k : P * (k + 1)],
                        rhs=codes[:].bitcast(FP8X4),
                        rhs_scale=plane[:],
                        start=True,
                        stop=True,
                    )
                k = bank * per_bank
                tile, k0 = total[(c, k)]
                part = tile[:, k - k0 : k - k0 + per_bank, :].rearrange("p k t -> p (k t)")
                if (c, bank) in SIDE:
                    sums = side.tile([P, BANK], F32, name="sums")
                    nc.scalar.copy(sums[:], acc[:])
                    nc.gpsimd.tensor_tensor(part, sums[:], part, ALU.add)
                else:
                    nc.vector.tensor_tensor(part, acc[:], part, ALU.add)
                k_end = k + per_bank
                count = 1 if c == 2 else 2
                if k_end % count == 0:
                    cols = slice(starts[c], starts[c] + width)
                    nc.sync.dma_start(
                        out_rows[:, k_end - count : k_end, cols], tile[:, k_end - count - k0 : k_end - k0, :]
                    )

        quantise_page(0)
        quantise_page(1)
        finish(0, range(3))
        quantise_page(2)
        finish(1, range(3))
        quantise_page(3)
        finish(2, range(N_TILES))
        finish(3, range(2))
        quantise_page(4)
        finish(3, range(2, N_TILES))
        finish(4, range(N_TILES))
